import numpy as np
import ml_dtypes


def mxq(x, axis, fmt="e4m3"):
    dtype, down = {"e4m3": (ml_dtypes.float8_e4m3fn, 7), "e5m2": (ml_dtypes.float8_e5m2, 14)}[fmt]
    v = np.moveaxis(np.asarray(x, np.float32).astype(ml_dtypes.bfloat16).astype(np.float64), axis, -1)
    blocks = v.reshape(v.shape[:-1] + (-1, 32))
    amax = np.abs(blocks).max(-1, keepdims=True)
    byte = np.maximum(np.where(amax > 0, np.frexp(amax)[1] - 1 + 127, 0) - down, 1)
    scale = np.exp2(byte - 127.0)
    codes = (blocks / scale).astype(np.float32).astype(dtype).astype(np.float64)
    return np.moveaxis((codes * scale).reshape(v.shape), -1, axis)


WIDE = False


def mx_kscale(k):
    if not WIDE:
        return np.ones(k)
    levels = np.array([10, -10, 5, -5, 0])
    if k % 512:
        return np.exp2(np.random.permutation(np.resize(levels, k // 32))).repeat(32)
    a = np.empty((k // 512, 16))
    for p in range(k // 512):
        a[p, :8] = np.random.permutation(np.resize(levels, 8))
        for g in range(8):
            far = levels[np.abs(levels - a[p, g]) >= 10]
            a[p, g + 8] = far[np.random.randint(len(far))]
    return np.exp2(a.ravel()).repeat(32)


def f64(x):
    return np.asarray(x).astype(np.float64)


def striped(idx):
    return np.tile(idx.reshape(-1, 16).T, (8, 1)).astype(np.uint16)


def unstriped(offs):
    return offs[:16].T.reshape(-1).astype(np.int64)


def pack_weight(w):
    k, n = w.shape
    w = f64(np.asarray(w, np.float32).astype(ml_dtypes.bfloat16)).reshape(k // 32, 32, n)
    amax = np.abs(w).max(1)
    byte = np.clip(np.where(amax > 0, np.frexp(amax)[1] - 1 + 127 - 7, 1), 1, 254)
    scaled = (w * np.exp2(127.0 - byte)[:, None, :]).reshape(k, n).astype(np.float32)
    words = np.ascontiguousarray(scaled.reshape(k // 512, 128, 4, n).transpose(0, 1, 3, 2)).astype(ml_dtypes.float8_e4m3fn).view(np.uint8)
    return words, np.ascontiguousarray(byte.astype(np.uint8).reshape(k // 512, 16, n))


def unpack_weight(words, scales):
    g, p, n, _ = words.shape
    vals = np.ascontiguousarray(words).view(ml_dtypes.float8_e4m3fn).astype(np.float64) * np.repeat(np.exp2(scales.astype(np.float64) - 127.0), 8, axis=1)[..., None]
    return vals.transpose(0, 1, 3, 2).reshape(g * 512, n)


def planes(y):
    n, m = y.shape
    v = y.astype(np.float32).astype(ml_dtypes.bfloat16).astype(np.float64).reshape(n // 32, 32, m)
    top = np.abs(v).max(1)
    byte = np.clip(np.where(top > 0, np.frexp(top)[1] - 1 + 127 - 7, 1), 1, 254)
    codes = (v * np.exp2(127.0 - byte)[:, None, :]).reshape(n, m).astype(np.float32).astype(ml_dtypes.float8_e4m3fn).view(np.uint8)
    words = codes.reshape(n // 512, 128, 4, m).transpose(0, 1, 3, 2)
    return np.ascontiguousarray(words), np.ascontiguousarray(byte.astype(np.uint8).reshape(n // 512, 16, m))


def relu(v):
    return np.maximum(v, 0.0)


K, T, S, H, N, W = 512, 1024, 512, 512, 512, 2048
P = 2 ** 7


def setup_inputs():
    n = np.random.standard_normal
    s = mx_kscale(K)[:, None]
    u = mx_kscale(H)
    packed_xT = pack_weight(n((K, T)) * s)
    packed_eT = pack_weight(n((K, W)) * s)
    return {
        "x_words": packed_xT[0],
        "x_scales": packed_xT[1],
        "e_words": packed_eT[0],
        "e_scales": packed_eT[1],
        "w1": (n((K, H)) / np.sqrt(2 * K) / s * u).astype(np.float32),
        "w2": (n((K, H)) / np.sqrt(2 * K) / s * u).astype(np.float32),
        "w3": (n((H, N)) / np.sqrt(H) / u[:, None]).astype(np.float32),
        "al": (np.tile(np.random.uniform(0.0, 1.0, S), (P, 1))).astype(np.float32),
        "be": (np.tile(np.random.uniform(0.0, 1.0, S), (P, 1))).astype(np.float32),
        "offs": striped(np.random.permutation(T)[:S]),
        "far": striped(np.random.permutation(T)[:S]),
        "fine": striped(np.random.permutation(W)[:S]),
        "ffar": striped(np.random.permutation(W)[:S]),
    }


def reference(x_words, x_scales, e_words, e_scales, w1, w2, w3, al, be, offs, far, fine, ffar):
    xq = unpack_weight(x_words, x_scales)[:, unstriped(offs)]
    w1q = mxq(f64(w1), 0, "e4m3")
    y = w1q.T @ xq
    x_far = unpack_weight(x_words, x_scales)[:, unstriped(far)]
    yf = w1q.T @ x_far
    e_fine = unpack_weight(e_words, e_scales)[:, unstriped(fine)]
    w2q = mxq(f64(w2), 0, "e4m3")
    p = w2q.T @ e_fine
    e_ffar = unpack_weight(e_words, e_scales)[:, unstriped(ffar)]
    pf = w2q.T @ e_ffar
    h = relu(y + f64(al)[:1] * (yf - y) + p + f64(be)[:1] * (pf - p))
    out_0 = mxq(f64(w3), 0, "e4m3").T @ mxq(h, 0, "e4m3")
    return (out_0,) + planes(out_0)

@@ -1,0 +1,251 @@
+from contextlib import ExitStack
+
+import concourse.mybir as mybir
+
+F32 = mybir.dt.float32
+BF16 = mybir.dt.bfloat16
+I32 = mybir.dt.int32
+U32 = mybir.dt.uint32
+U16 = mybir.dt.uint16
+U8 = mybir.dt.uint8
+FP8X4 = mybir.dt.float8_e4m3fn_x4
+ALU = mybir.AluOpType
+ACT = mybir.ActivationFunctionType
+
+P = 128
+PACK = 4
+K = 512
+S = 512
+TILES = S // P
+HALF = S // 2
+
+FLOPS = 5 * 2 * K * K * S
+BYTES = (1024 + 2048) * (K + K // 32) + 3 * K * K * 4 + 2 * S * 4 + 4 * P * (S // 16) * 2 + K * S * 4 + K * S + K * S // 32
+
+
+def tile_picked_yngp_none_po_kernel(
+    tc, x_words, x_scales, e_words, e_scales, w1, w2, w3, al, be, offs, far, fine, ffar, out_0, out_1, out_2
+):
+    nc = tc.nc
+    with ExitStack() as ctx:
+        keep = ctx.enter_context(tc.tile_pool(name="keep", bufs=1))
+        psum = ctx.enter_context(tc.psum_pool(name="psum", bufs=1))
+
+        def sb(name, shape, dtype, tag=None):
+            return keep.tile(shape, dtype, name=name, tag=tag or name, align_bytes=64)
+
+        def bank(tag):
+            return psum.tile([P, K], F32, name=tag, tag=tag)
+
+
+        def table_tiles(name, words):
+            cols = words.shape[2]
+            wt = sb(name + "_words", [P, cols], I32)
+            st = sb(name + "_scales", [P, cols], U8)
+            nc.vector.memset(st[:].bitcast(I32), 0)
+            return wt, st
+
+        def load_words(wt, words):
+            nc.sync.dma_start(out=wt[:], in_=words[0].rearrange("p c r -> p (c r)").bitcast(I32))
+
+        def load_scales(st, scales):
+            for q in range(4):
+                nc.sync.dma_start(out=st[32 * q : 32 * q + 4, :].bitcast(I32), in_=scales[0, 4 * q : 4 * q + 4, :].bitcast(I32))
+
+        def load_list(name, lst):
+            lt = keep.tile([P, S // 16], U16, name=name)
+            nc.sync.dma_start(lt[:], lst)
+            return lt
+
+        def load_weight(name, w, c0, c1):
+            raw = sb(name, [P, PACK, c1 - c0], F32)
+            nc.sync.dma_start(out=raw[:], in_=w.rearrange("(p j) c -> p j c", j=PACK)[:, :, c0:c1])
+            return raw
+
+        xw, xs = table_tiles("x", x_words)
+        ew, es = table_tiles("e", e_words)
+        ab_rows = sb("ab_rows", [P, P], F32)
+        nc.vector.memset(ab_rows[:], 0.0)
+        ones = sb("ones", [P, P], F32)
+        nc.vector.memset(ones[:], 1.0)
+        column = sb("column", [P, P], F32)
+        nc.vector.tensor_tensor_scan(column[:], ones[:], ones[:], -1.0, ALU.mult, ALU.add)
+        turned = sb("turned", [P, P], F32)
+        nc.vector.transpose(turned[:], column[:])
+        ident = sb("ident", [P, P], F32)
+        for q in range(4):
+            rows = slice(32 * q, 32 * q + 32)
+            nc.vector.tensor_scalar(ident[rows, :], column[rows, :], turned[rows, 32 * q : 32 * q + 1], None, ALU.is_equal)
+
+        l_offs = load_list("l_offs", offs)
+        load_words(xw, x_words)
+        load_scales(xs, x_scales)
+        l_far = load_list("l_far", far)
+        w1_raw = [load_weight("w1_raw%d" % h, w1, h * HALF, (h + 1) * HALF) for h in range(2)]
+        nc.sync.dma_start(out=ab_rows[0:TILES, :], in_=al[0:1, :].rearrange("o (t c) -> (o t) c", c=P))
+        nc.sync.dma_start(out=ab_rows[TILES : 2 * TILES, :], in_=be[0:1, :].rearrange("o (t c) -> (o t) c", c=P))
+        w2_raw = [load_weight("w2_raw%d" % h, w2, h * HALF, (h + 1) * HALF) for h in range(2)]
+        load_scales(es, e_scales)
+        load_words(ew, e_words)
+        l_fine = load_list("l_fine", fine)
+        l_ffar = load_list("l_ffar", ffar)
+        w3_raw = load_weight("w3_raw", w3, 0, K)
+
+        ab_ps = bank("prod0")
+        nc.tensor.transpose(ab_ps[:, 0:P], ab_rows[:], ident[:])
+        far_wt = sb("far_wt", [P, 2 * TILES], F32)
+        near_wt = sb("near_wt", [P, 2 * TILES], F32)
+        nc.scalar.copy(far_wt[:], ab_ps[:, 0 : 2 * TILES])
+        nc.scalar.activation(near_wt[:], ab_ps[:, 0 : 2 * TILES], ACT.Copy, bias=1.0, scale=-1.0)
+
+        def gather(name, wt, st, lt, h, tag=None):
+            gw = sb("%s_w%d" % (name, h), [P, HALF], U32, tag)
+            gs = sb("%s_s%d" % (name, h), [P, HALF], U8)
+            cols = lt[:, h * (HALF // 16) : (h + 1) * (HALF // 16)]
+            nc.vector.tensor_copy(gw[:], wt[:].bitcast(U32).indirect(cols))
+            nc.vector.tensor_copy(gs[:], st[:].indirect(cols))
+            return gw, gs
+
+        def quantize(name, src, cols):
+            codes = sb(name + "_codes", [P, cols], U32)
+            scales = sb(name + "_bytes", [P, cols], U8)
+            nc.vector.quantize_mx(out=codes[:].bitcast(FP8X4), scales=scales[:], in_=src)
+            return codes, scales
+
+        def round_half(copy, wb, raws, h):
+            copy(
+                wb[:, h * HALF * PACK : (h + 1) * HALF * PACK].rearrange("p (c i j) -> p c j i", i=4, j=PACK),
+                raws[h][:].rearrange("p j (c i) -> p c j i", i=4),
+            )
+
+        picked = {}
+        picked["y", 0] = gather("y", xw, xs, l_offs, 0)
+        picked["yf", 0] = gather("yf", xw, xs, l_far, 0)
+        picked["y", 1] = gather("y", xw, xs, l_offs, 1)
+        w1_b = sb("w1_b", [P, K * PACK], BF16)
+        round_half(nc.scalar.copy, w1_b, w1_raw, 0)
+        round_half(nc.scalar.copy, w1_b, w1_raw, 1)
+        w1_q = quantize("w1", w1_b[:], K)
+        picked["yf", 1] = gather("yf", xw, xs, l_far, 1, "w1_b")
+        w2_b = sb("w2_b", [P, K * PACK], BF16)
+        round_half(nc.scalar.copy, w2_b, w2_raw, 0)
+        round_half(nc.vector.tensor_copy, w2_b, w2_raw, 1)
+        w2_q = quantize("w2", w2_b[:], K)
+        for h in range(2):
+            picked["p", h] = gather("p", ew, es, l_fine, h)
+            picked["pf", h] = gather("pf", ew, es, l_ffar, h)
+
+        def product(name, wq, t, tag):
+            gw, gs = picked[name, t // 2]
+            cols = slice((t % 2) * P, (t % 2 + 1) * P)
+            acc = bank(tag)
+            nc.tensor.matmul_mx(
+                out=acc[:], lhsT=gw[:, cols].bitcast(FP8X4), lhsT_scale=gs[:, cols],
+                rhs=wq[0][:].bitcast(FP8X4), rhs_scale=wq[1][:], start=True, stop=True,
+            )
+            return acc[:].rearrange("p (m r) -> p r m", r=PACK)
+
+        def scaled(name, wq, wt, t, tag):
+            acc = product(name, wq, t, tag)
+            term = sb("%s_term%d" % (name, t), [P, PACK, P], F32)
+            nc.scalar.activation(term[:], acc, ACT.Copy, scale=wt)
+            return term
+
+        def scaled_onto(name, wq, wt, t, tag, other, after):
+            acc = product(name, wq, t, tag)
+            term = sb("%s_term%d" % (name, t), [P, PACK, P], F32, after)
+            nc.vector.scalar_tensor_tensor(term[:], acc, wt, other[:], ALU.mult, ALU.add)
+            return term
+
+        def turn_into(acc, term, first, last):
+            for r in range(PACK):
+                nc.tensor.matmul(
+                    acc[:, r * P : (r + 1) * P], lhsT=term[:, r, :], rhs=ident[:], is_transpose=True,
+                    start=(first and r == 0), stop=(last and r == PACK - 1),
+                )
+
+        out_codes = sb("out_codes", [P, S], I32)
+        out_bytes = sb("out_bytes", [P, S], U8)
+        out_rows = out_0.rearrange("(p r) j -> p r j", r=PACK)
+        out_words = out_1[0].rearrange("p c r -> p (c r)").bitcast(I32)
+
+        sums = {}
+        near = {}
+        other = {}
+        h_q = {}
+        w3_q = []
+
+        def hidden(t):
+            hb = sb("h_b%d" % t, [P, P, PACK], BF16)
+            nc.scalar.activation(hb[:], sums[t][:].rearrange("p (r j) -> p j r", r=PACK), ACT.Relu)
+            h_q[t] = quantize("h%d" % t, hb[:].rearrange("p j r -> p (j r)"), P)
+
+        def last(t):
+            acc = bank("sum%d" % t)
+            for r in range(PACK):
+                cols = slice(r * P, (r + 1) * P)
+                nc.tensor.matmul_mx(
+                    out=acc[:, cols], lhsT=w3_q[0][:, cols].bitcast(FP8X4), lhsT_scale=w3_q[1][:, cols],
+                    rhs=h_q[t][0][:].bitcast(FP8X4), rhs_scale=h_q[t][1][:], start=True, stop=True,
+                )
+            res = sb("res%d" % t, [P, PACK, P], F32)
+            nc.scalar.copy(res[:].rearrange("p r j -> p (r j)"), acc[:])
+            cols = slice(t * P, (t + 1) * P)
+            nc.sync.dma_start(out=out_rows[:, :, cols], in_=res[:])
+            rb = sb("res_b%d" % t, [P, P * PACK], BF16)
+            nc.vector.tensor_copy(
+                rb[:].rearrange("p (c i r) -> p c r i", i=4, r=PACK), res[:].rearrange("p r (c i) -> p c r i", i=4)
+            )
+            nc.vector.quantize_mx(out=out_codes[:, cols].bitcast(FP8X4), scales=out_bytes[:, cols], in_=rb[:])
+            if t % 2 == 1:
+                pair = slice((t - 1) * P, (t + 1) * P)
+                nc.sync.dma_start(out=out_words[:, pair], in_=out_codes[:, pair])
+
+        for t in range(TILES):
+            kind = "prod" if t < 2 else "sum"
+            near[t] = scaled("y", w1_q, near_wt[:, t : t + 1], t, "%s%d" % (kind, 2 * (t % 2)))
+            other[t] = scaled("yf", w1_q, far_wt[:, t : t + 1], t, "%s%d" % (kind, 2 * (t % 2) + 1))
+        for t in range(TILES):
+            sums[t] = bank("sum%d" % t)
+        for t in range(2):
+            turn_into(sums[t], near[t], True, False)
+            turn_into(sums[t], other[t], False, False)
+        turn_into(sums[2], other[2], True, False)
+
+        def p_wt(t):
+            return near_wt[:, TILES + t : TILES + t + 1]
+
+        def pf_wt(t):
+            return far_wt[:, TILES + t : TILES + t + 1]
+
+        fine_terms = []
+        for t in range(2):
+            fine_terms.append(scaled("p", w2_q, p_wt(t), t, "prod%d" % (2 * t)))
+            fine_terms.append(scaled("pf", w2_q, pf_wt(t), t, "prod%d" % (2 * t + 1)))
+        w3_b = sb("w3_b", [P, K * PACK], BF16)
+        nc.vector.tensor_copy(
+            w3_b[:].rearrange("p (r m j) -> p m j r", r=PACK, j=PACK), w3_raw[:].rearrange("p j (m r) -> p m j r", r=PACK)
+        )
+        w3_q.extend(quantize("w3", w3_b[:], K))
+        for t in range(2):
+            turn_into(sums[t], fine_terms[2 * t], False, False)
+            turn_into(sums[t], fine_terms[2 * t + 1], False, True)
+            hidden(t)
+        u2 = scaled_onto("p", w2_q, p_wt(2), 2, "prod0", near[2], "w3_raw")
+        v2 = scaled("pf", w2_q, pf_wt(2), 2, "prod1")
+        u3 = scaled_onto("p", w2_q, p_wt(3), 3, "prod2", near[3], "w3_b")
+        v3 = scaled_onto("pf", w2_q, pf_wt(3), 3, "prod3", other[3], None)
+        turn_into(sums[2], v2, False, False)
+        turn_into(sums[2], u2, False, True)
+        last(0)
+        hidden(2)
+        turn_into(sums[3], u3, True, False)
+        turn_into(sums[3], v3, False, True)
+        last(1)
+        hidden(3)
+        last(2)
+        last(3)
+
+        for q in range(4):
+            eng = nc.sync if q % 2 == 0 else nc.scalar
+            eng.dma_start(out=out_2[0, 4 * q : 4 * q + 4, :].bitcast(I32), in_=out_bytes[32 * q : 32 * q + 4, :].bitcast(I32))

@@ -106,8 +106,8 @@ def tile_picked_yngp_none_po_kernel(
             nc.vector.tensor_copy(gs[:], st[:].indirect(cols))
             return gw, gs
 
-        def quantize(name, src, cols):
-            codes = sb(name + "_codes", [P, cols], U32)
+        def quantize(name, src, cols, tag=None):
+            codes = sb(name + "_codes", [P, cols], U32, tag)
             scales = sb(name + "_bytes", [P, cols], U8)
             nc.vector.quantize_mx(out=codes[:].bitcast(FP8X4), scales=scales[:], in_=src)
             return codes, scales
@@ -178,7 +178,7 @@ def tile_picked_yngp_none_po_kernel(
         def hidden(t):
             hb = sb("h_b%d" % t, [P, P, PACK], BF16)
             nc.scalar.activation(hb[:], sums[t][:].rearrange("p (r j) -> p j r", r=PACK), ACT.Relu)
-            h_q[t] = quantize("h%d" % t, hb[:].rearrange("p j r -> p (j r)"), P)
+            h_q[t] = quantize("h%d" % t, hb[:].rearrange("p j r -> p (j r)"), P, {1: "w3_b0", 2: "w3_b1"}.get(t))
 
         def last(t):
             acc = bank("sum%d" % t)
@@ -201,16 +201,11 @@ def tile_picked_yngp_none_po_kernel(
                 pair = slice((t - 1) * P, (t + 1) * P)
                 nc.sync.dma_start(out=out_words[:, pair], in_=out_codes[:, pair])
 
-        for t in range(TILES):
-            kind = "prod" if t < 2 else "sum"
-            near[t] = scaled("y", w1_q, near_wt[:, t : t + 1], t, "%s%d" % (kind, 2 * (t % 2)))
-            other[t] = scaled("yf", w1_q, far_wt[:, t : t + 1], t, "%s%d" % (kind, 2 * (t % 2) + 1))
-        for t in range(TILES):
-            sums[t] = bank("sum%d" % t)
-        for t in range(2):
-            turn_into(sums[t], near[t], True, False)
-            turn_into(sums[t], other[t], False, False)
-        turn_into(sums[2], other[2], True, False)
+        def y_wt(t):
+            return near_wt[:, t : t + 1]
+
+        def yf_wt(t):
+            return far_wt[:, t : t + 1]
 
         def p_wt(t):
             return near_wt[:, TILES + t : TILES + t + 1]
@@ -218,33 +213,48 @@ def tile_picked_yngp_none_po_kernel(
         def pf_wt(t):
             return far_wt[:, TILES + t : TILES + t + 1]
 
+        for t in range(2):
+            near[t] = scaled("y", w1_q, y_wt(t), t, "sum%d" % (2 * t))
+            other[t] = scaled("yf", w1_q, yf_wt(t), t, "sum%d" % (2 * t + 1))
+        for t in range(2, TILES):
+            other[t] = scaled("yf", w1_q, yf_wt(t), t, "prod%d" % (t - 2))
+        for t in range(2, TILES):
+            near[t] = scaled("y", w1_q, y_wt(t), t, "prod%d" % t)
+        for t in range(TILES):
+            sums[t] = bank("sum%d" % t)
+            turn_into(sums[t], other[t], True, False)
+            if t < 2:
+                turn_into(sums[t], near[t], False, False)
+
         fine_terms = []
         for t in range(2):
             fine_terms.append(scaled("p", w2_q, p_wt(t), t, "prod%d" % (2 * t)))
             fine_terms.append(scaled("pf", w2_q, pf_wt(t), t, "prod%d" % (2 * t + 1)))
-        w3_b = sb("w3_b", [P, K * PACK], BF16)
-        nc.vector.tensor_copy(
-            w3_b[:].rearrange("p (r m j) -> p m j r", r=PACK, j=PACK), w3_raw[:].rearrange("p j (m r) -> p m j r", r=PACK)
-        )
-        w3_q.extend(quantize("w3", w3_b[:], K))
+        fused = {}
+        for t in range(2, TILES):
+            u = scaled_onto("p", w2_q, p_wt(t), t, "prod%d" % (2 * t - 4), near[t], None)
+            fused[t] = scaled_onto("pf", w2_q, pf_wt(t), t, "prod%d" % (2 * t - 3), u, None)
+        w3_codes = sb("w3_codes", [P, K], U32)
+        w3_bytes = sb("w3_bytes", [P, K], U8)
+        w3_q.extend([w3_codes, w3_bytes])
+        w3_dealt = w3_raw[:].rearrange("p j (m r) -> p r m j", r=PACK)
+        for h in range(2):
+            w3_b = sb("w3_b%d" % h, [P, 2, P, PACK], BF16)
+            for r in range(2):
+                nc.gpsimd.tensor_scalar(w3_b[:, r], w3_dealt[:, 2 * h + r], 1.0, 0.0, ALU.mult, ALU.add)
+            cols = slice(h * HALF, (h + 1) * HALF)
+            nc.vector.quantize_mx(
+                out=w3_codes[:, cols].bitcast(FP8X4), scales=w3_bytes[:, cols], in_=w3_b[:].rearrange("p r m j -> p (r m j)")
+            )
         for t in range(2):
             turn_into(sums[t], fine_terms[2 * t], False, False)
             turn_into(sums[t], fine_terms[2 * t + 1], False, True)
+        for t in range(2, TILES):
+            turn_into(sums[t], fused[t], False, True)
+        for t in range(TILES):
             hidden(t)
-        u2 = scaled_onto("p", w2_q, p_wt(2), 2, "prod0", near[2], "w3_raw")
-        v2 = scaled("pf", w2_q, pf_wt(2), 2, "prod1")
-        u3 = scaled_onto("p", w2_q, p_wt(3), 3, "prod2", near[3], "w3_b")
-        v3 = scaled_onto("pf", w2_q, pf_wt(3), 3, "prod3", other[3], None)
-        turn_into(sums[2], v2, False, False)
-        turn_into(sums[2], u2, False, True)
-        last(0)
-        hidden(2)
-        turn_into(sums[3], u3, True, False)
-        turn_into(sums[3], v3, False, True)
-        last(1)
-        hidden(3)
-        last(2)
-        last(3)
+        for t in range(TILES):
+            last(t)
 
         for q in range(4):
             eng = nc.sync if q % 2 == 0 else nc.scalar

@@ -81,15 +81,15 @@ def tile_picked_yngp_none_po_kernel(
         load_words(xw, x_words)
         load_scales(xs, x_scales)
         l_far = load_list("l_far", far)
-        w1_raw = [load_weight("w1_raw%d" % h, w1, h * HALF, (h + 1) * HALF) for h in range(2)]
+        w1_raw = load_weight("w1_raw", w1, 0, K)
         nc.sync.dma_start(out=ab_rows[0:TILES, :], in_=al[0:1, :].rearrange("o (t c) -> (o t) c", c=P))
         nc.sync.dma_start(out=ab_rows[TILES : 2 * TILES, :], in_=be[0:1, :].rearrange("o (t c) -> (o t) c", c=P))
-        w2_raw = [load_weight("w2_raw%d" % h, w2, h * HALF, (h + 1) * HALF) for h in range(2)]
-        load_scales(es, e_scales)
-        load_words(ew, e_words)
         l_fine = load_list("l_fine", fine)
+        load_words(ew, e_words)
+        load_scales(es, e_scales)
         l_ffar = load_list("l_ffar", ffar)
-        w3_raw = load_weight("w3_raw", w3, 0, K)
+        w2_raw = [load_weight("w2_raw%d" % h, w2, h * HALF, (h + 1) * HALF) for h in range(2)]
+        w3_raw = [load_weight("w3_raw%d" % h, w3, h * HALF, (h + 1) * HALF) for h in range(2)]
 
         ab_ps = bank("prod0")
         nc.tensor.transpose(ab_ps[:, 0:P], ab_rows[:], ident[:])
@@ -98,13 +98,15 @@ def tile_picked_yngp_none_po_kernel(
         nc.scalar.copy(far_wt[:], ab_ps[:, 0 : 2 * TILES])
         nc.scalar.activation(near_wt[:], ab_ps[:, 0 : 2 * TILES], ACT.Copy, bias=1.0, scale=-1.0)
 
-        def gather(name, wt, st, lt, h, tag=None):
-            gw = sb("%s_w%d" % (name, h), [P, HALF], U32, tag)
-            gs = sb("%s_s%d" % (name, h), [P, HALF], U8)
-            cols = lt[:, h * (HALF // 16) : (h + 1) * (HALF // 16)]
-            nc.vector.tensor_copy(gw[:], wt[:].bitcast(U32).indirect(cols))
-            nc.vector.tensor_copy(gs[:], st[:].indirect(cols))
-            return gw, gs
+        def gather_words(name, wt, lt, j0, j1, tag=None):
+            gw = sb("%s_w%d" % (name, j0), [P, j1 - j0], U32, tag)
+            nc.vector.tensor_copy(gw[:], wt[:].bitcast(U32).indirect(lt[:, j0 // 16 : j1 // 16]))
+            return gw
+
+        def gather_bytes(name, st, lt, j0, j1, tag=None):
+            gs = sb("%s_s%d" % (name, j0), [P, j1 - j0], U8, tag)
+            nc.vector.tensor_copy(gs[:], st[:].indirect(lt[:, j0 // 16 : j1 // 16]))
+            return gs
 
         def quantize(name, src, cols, tag=None):
             codes = sb(name + "_codes", [P, cols], U32, tag)
@@ -112,32 +114,35 @@ def tile_picked_yngp_none_po_kernel(
             nc.vector.quantize_mx(out=codes[:].bitcast(FP8X4), scales=scales[:], in_=src)
             return codes, scales
 
-        def round_half(copy, wb, raws, h):
-            copy(
-                wb[:, h * HALF * PACK : (h + 1) * HALF * PACK].rearrange("p (c i j) -> p c j i", i=4, j=PACK),
-                raws[h][:].rearrange("p j (c i) -> p c j i", i=4),
-            )
+        def round_on_gpsimd(dst, src):
+            nc.gpsimd.tensor_scalar(dst, src, 1.0, 0.0, ALU.mult, ALU.add)
+
+        def half_columns(wb, h):
+            return wb[:, h * HALF * PACK : (h + 1) * HALF * PACK]
 
         picked = {}
-        picked["y", 0] = gather("y", xw, xs, l_offs, 0)
-        picked["yf", 0] = gather("yf", xw, xs, l_far, 0)
-        picked["y", 1] = gather("y", xw, xs, l_offs, 1)
+        picked["y", 0] = (gather_words("y", xw, l_offs, 0, S), gather_bytes("y", xs, l_offs, 0, S))
+        yf_words = gather_words("yf", xw, l_far, 0, S)
         w1_b = sb("w1_b", [P, K * PACK], BF16)
-        round_half(nc.scalar.copy, w1_b, w1_raw, 0)
-        round_half(nc.scalar.copy, w1_b, w1_raw, 1)
+        nc.scalar.copy(
+            half_columns(w1_b, 0).rearrange("p (c i j) -> p c j i", i=4, j=PACK),
+            w1_raw[:, :, 0:HALF].rearrange("p j (c i) -> p c j i", i=4),
+        )
+        round_on_gpsimd(half_columns(w1_b, 1).rearrange("p (c j) -> p c j", j=PACK), w1_raw[:, :, HALF:K].rearrange("p j c -> p c j"))
         w1_q = quantize("w1", w1_b[:], K)
-        picked["yf", 1] = gather("yf", xw, xs, l_far, 1, "w1_b")
+        picked["yf", 0] = (yf_words, gather_bytes("yf", xs, l_far, 0, S, "w1_b"))
+        picked["p", 0] = (gather_words("p", ew, l_fine, 0, S), gather_bytes("p", es, l_fine, 0, S))
+        pf_words = gather_words("pf", ew, l_ffar, 0, S)
         w2_b = sb("w2_b", [P, K * PACK], BF16)
-        round_half(nc.scalar.copy, w2_b, w2_raw, 0)
-        round_half(nc.vector.tensor_copy, w2_b, w2_raw, 1)
-        w2_q = quantize("w2", w2_b[:], K)
         for h in range(2):
-            picked["p", h] = gather("p", ew, es, l_fine, h)
-            picked["pf", h] = gather("pf", ew, es, l_ffar, h)
+            round_on_gpsimd(half_columns(w2_b, h).rearrange("p (c j) -> p c j", j=PACK), w2_raw[h][:].rearrange("p j c -> p c j"))
+        w2_q = quantize("w2", w2_b[:], K)
+        picked["pf", 0] = (pf_words, gather_bytes("pf", es, l_ffar, 0, S, "w2_b"))
 
         def product(name, wq, t, tag):
-            gw, gs = picked[name, t // 2]
-            cols = slice((t % 2) * P, (t % 2 + 1) * P)
+            j0 = max(j for n, j in picked if n == name and j <= t * P)
+            gw, gs = picked[name, j0]
+            cols = slice(t * P - j0, (t + 1) * P - j0)
             acc = bank(tag)
             nc.tensor.matmul_mx(
                 out=acc[:], lhsT=gw[:, cols].bitcast(FP8X4), lhsT_scale=gs[:, cols],
@@ -145,16 +150,16 @@ def tile_picked_yngp_none_po_kernel(
             )
             return acc[:].rearrange("p (m r) -> p r m", r=PACK)
 
-        def scaled(name, wq, wt, t, tag):
+        def scaled(name, wq, wt, t, tag, term=None):
             acc = product(name, wq, t, tag)
-            term = sb("%s_term%d" % (name, t), [P, PACK, P], F32)
-            nc.scalar.activation(term[:], acc, ACT.Copy, scale=wt)
+            if term is None:
+                term = sb("%s_term%d" % (name, t), [P, PACK, P], F32)[:]
+            nc.scalar.activation(term, acc, ACT.Copy, scale=wt)
             return term
 
-        def scaled_onto(name, wq, wt, t, tag, other, after):
+        def scaled_onto(name, wq, wt, t, tag, other, term):
             acc = product(name, wq, t, tag)
-            term = sb("%s_term%d" % (name, t), [P, PACK, P], F32, after)
-            nc.vector.scalar_tensor_tensor(term[:], acc, wt, other[:], ALU.mult, ALU.add)
+            nc.vector.scalar_tensor_tensor(term, acc, wt, other, ALU.mult, ALU.add)
             return term
 
         def turn_into(acc, term, first, last):
@@ -169,6 +174,7 @@ def tile_picked_yngp_none_po_kernel(
         out_rows = out_0.rearrange("(p r) j -> p r j", r=PACK)
         out_words = out_1[0].rearrange("p c r -> p (c r)").bitcast(I32)
 
+        res_b = [sb("res_b%d" % h, [P, 2, P * PACK], BF16) for h in range(2)]
         sums = {}
         near = {}
         other = {}
@@ -178,7 +184,9 @@ def tile_picked_yngp_none_po_kernel(
         def hidden(t):
             hb = sb("h_b%d" % t, [P, P, PACK], BF16)
             nc.scalar.activation(hb[:], sums[t][:].rearrange("p (r j) -> p j r", r=PACK), ACT.Relu)
-            h_q[t] = quantize("h%d" % t, hb[:].rearrange("p j r -> p (j r)"), P, {1: "w3_b0", 2: "w3_b1"}.get(t))
+            h_bytes = sb("h_bytes%d" % t, [P, P], U8)
+            nc.vector.quantize_mx(out=h_codes[t].bitcast(FP8X4), scales=h_bytes[:], in_=hb[:].rearrange("p j r -> p (j r)"))
+            h_q[t] = (h_codes[t], h_bytes[:])
 
         def last(t):
             acc = bank("sum%d" % t)
@@ -186,19 +194,21 @@ def tile_picked_yngp_none_po_kernel(
                 cols = slice(r * P, (r + 1) * P)
                 nc.tensor.matmul_mx(
                     out=acc[:, cols], lhsT=w3_q[0][:, cols].bitcast(FP8X4), lhsT_scale=w3_q[1][:, cols],
-                    rhs=h_q[t][0][:].bitcast(FP8X4), rhs_scale=h_q[t][1][:], start=True, stop=True,
+                    rhs=h_q[t][0].bitcast(FP8X4), rhs_scale=h_q[t][1], start=True, stop=True,
                 )
             res = sb("res%d" % t, [P, PACK, P], F32)
             nc.scalar.copy(res[:].rearrange("p r j -> p (r j)"), acc[:])
             cols = slice(t * P, (t + 1) * P)
             nc.sync.dma_start(out=out_rows[:, :, cols], in_=res[:])
-            rb = sb("res_b%d" % t, [P, P * PACK], BF16)
+            rb = res_b[t // 2]
             nc.vector.tensor_copy(
-                rb[:].rearrange("p (c i r) -> p c r i", i=4, r=PACK), res[:].rearrange("p r (c i) -> p c r i", i=4)
+                rb[:, t % 2].rearrange("p (c i r) -> p c r i", i=4, r=PACK), res[:].rearrange("p r (c i) -> p c r i", i=4)
             )
-            nc.vector.quantize_mx(out=out_codes[:, cols].bitcast(FP8X4), scales=out_bytes[:, cols], in_=rb[:])
             if t % 2 == 1:
                 pair = slice((t - 1) * P, (t + 1) * P)
+                nc.vector.quantize_mx(
+                    out=out_codes[:, pair].bitcast(FP8X4), scales=out_bytes[:, pair], in_=rb[:].rearrange("p a n -> p (a n)")
+                )
                 nc.sync.dma_start(out=out_words[:, pair], in_=out_codes[:, pair])
 
         def y_wt(t):
@@ -214,42 +224,45 @@ def tile_picked_yngp_none_po_kernel(
             return far_wt[:, TILES + t : TILES + t + 1]
 
         for t in range(2):
-            near[t] = scaled("y", w1_q, y_wt(t), t, "sum%d" % (2 * t))
-            other[t] = scaled("yf", w1_q, yf_wt(t), t, "sum%d" % (2 * t + 1))
+            near[t] = scaled("y", w1_q, y_wt(t), t, "sum%d" % t)
+        for t in range(2):
+            other[t] = scaled("yf", w1_q, yf_wt(t), t, "sum%d" % (2 + t))
         for t in range(2, TILES):
-            other[t] = scaled("yf", w1_q, yf_wt(t), t, "prod%d" % (t - 2))
-        for t in range(2, TILES):
-            near[t] = scaled("y", w1_q, y_wt(t), t, "prod%d" % t)
-        for t in range(TILES):
-            sums[t] = bank("sum%d" % t)
-            turn_into(sums[t], other[t], True, False)
-            if t < 2:
-                turn_into(sums[t], near[t], False, False)
+            near[t] = scaled("y", w1_q, y_wt(t), t, "prod%d" % (2 * t - 4))
+            other[t] = scaled("yf", w1_q, yf_wt(t), t, "prod%d" % (2 * t - 3))
 
-        fine_terms = []
+        def coarse_sum(t):
+            sums[t] = bank("sum%d" % t)
+            turn_into(sums[t], near[t], True, False)
+            turn_into(sums[t], other[t], False, False)
+
         for t in range(2):
-            fine_terms.append(scaled("p", w2_q, p_wt(t), t, "prod%d" % (2 * t)))
-            fine_terms.append(scaled("pf", w2_q, pf_wt(t), t, "prod%d" % (2 * t + 1)))
+            coarse_sum(t)
+
+        w3_b = sb("w3_b", [P, PACK, 2, P // 2, PACK], BF16)
+        for r in range(PACK):
+            round_on_gpsimd(w3_b[:, r, 0], w3_raw[0][:].rearrange("p j (m r) -> p r m j", r=PACK)[:, r])
+        nc.vector.tensor_copy(w3_b[:, :, 1].rearrange("p r m j -> p m j r"), w3_raw[1][:].rearrange("p j (m r) -> p m j r", r=PACK))
+
+        fine_near = {}
         fused = {}
+        fine_sums = sb("fine_sums", [P, TILES, PACK, P], F32, "w3_raw1")
+
+        def fine_pair(t0):
+            for t in (t0, t0 + 1):
+                fine_near[t] = scaled("p", w2_q, p_wt(t), t, "prod%d" % (t % 2))
+            for t in (t0, t0 + 1):
+                fused[t] = scaled_onto("pf", w2_q, pf_wt(t), t, "prod%d" % (2 + t % 2), fine_near[t], fine_sums[:, t])
+
+        fine_pair(0)
         for t in range(2, TILES):
-            u = scaled_onto("p", w2_q, p_wt(t), t, "prod%d" % (2 * t - 4), near[t], None)
-            fused[t] = scaled_onto("pf", w2_q, pf_wt(t), t, "prod%d" % (2 * t - 3), u, None)
-        w3_codes = sb("w3_codes", [P, K], U32)
-        w3_bytes = sb("w3_bytes", [P, K], U8)
-        w3_q.extend([w3_codes, w3_bytes])
-        w3_dealt = w3_raw[:].rearrange("p j (m r) -> p r m j", r=PACK)
-        for h in range(2):
-            w3_b = sb("w3_b%d" % h, [P, 2, P, PACK], BF16)
-            for r in range(2):
-                nc.gpsimd.tensor_scalar(w3_b[:, r], w3_dealt[:, 2 * h + r], 1.0, 0.0, ALU.mult, ALU.add)
-            cols = slice(h * HALF, (h + 1) * HALF)
-            nc.vector.quantize_mx(
-                out=w3_codes[:, cols].bitcast(FP8X4), scales=w3_bytes[:, cols], in_=w3_b[:].rearrange("p r m j -> p (r m j)")
-            )
-        for t in range(2):
-            turn_into(sums[t], fine_terms[2 * t], False, False)
-            turn_into(sums[t], fine_terms[2 * t + 1], False, True)
-        for t in range(2, TILES):
+            coarse_sum(t)
+        fine_pair(2)
+        w3_q.extend(quantize("w3", w3_b[:].rearrange("p r h m j -> p (r h m j)"), K))
+        h_codes = [sb("h_codes0", [P, P], U32)[:]]
+        h_later = sb("h_later", [P, TILES - 1, P], U32, "w3_b")
+        h_codes.extend([h_later[:, t] for t in range(TILES - 1)])
+        for t in range(TILES):
             turn_into(sums[t], fused[t], False, True)
         for t in range(TILES):
             hidden(t)

from contextlib import ExitStack

import concourse.mybir as mybir

F32 = mybir.dt.float32
BF16 = mybir.dt.bfloat16
I32 = mybir.dt.int32
U32 = mybir.dt.uint32
U16 = mybir.dt.uint16
U8 = mybir.dt.uint8
FP8X4 = mybir.dt.float8_e4m3fn_x4
ALU = mybir.AluOpType
ACT = mybir.ActivationFunctionType

P = 128
PACK = 4
K = 512
S = 512
TILES = S // P
HALF = S // 2

FLOPS = 5 * 2 * K * K * S
BYTES = (1024 + 2048) * (K + K // 32) + 3 * K * K * 4 + 2 * S * 4 + 4 * P * (S // 16) * 2 + K * S * 4 + K * S + K * S // 32


def tile_picked_yngp_none_po_kernel(
    tc, x_words, x_scales, e_words, e_scales, w1, w2, w3, al, be, offs, far, fine, ffar, out_0, out_1, out_2
):
    nc = tc.nc
    with ExitStack() as ctx:
        keep = ctx.enter_context(tc.tile_pool(name="keep", bufs=1))
        psum = ctx.enter_context(tc.psum_pool(name="psum", bufs=1))

        def sb(name, shape, dtype, tag=None):
            return keep.tile(shape, dtype, name=name, tag=tag or name, align_bytes=64)

        def bank(tag):
            return psum.tile([P, K], F32, name=tag, tag=tag)


        def table_tiles(name, words):
            cols = words.shape[2]
            wt = sb(name + "_words", [P, cols], I32)
            st = sb(name + "_scales", [P, cols], U8)
            nc.vector.memset(st[:].bitcast(I32), 0)
            return wt, st

        def load_words(wt, words):
            nc.sync.dma_start(out=wt[:], in_=words[0].rearrange("p c r -> p (c r)").bitcast(I32))

        def load_scales(st, scales):
            for q in range(4):
                nc.sync.dma_start(out=st[32 * q : 32 * q + 4, :].bitcast(I32), in_=scales[0, 4 * q : 4 * q + 4, :].bitcast(I32))

        def load_list(name, lst):
            lt = keep.tile([P, S // 16], U16, name=name)
            nc.sync.dma_start(lt[:], lst)
            return lt

        def load_weight(name, w, c0, c1):
            raw = sb(name, [P, PACK, c1 - c0], F32)
            nc.sync.dma_start(out=raw[:], in_=w.rearrange("(p j) c -> p j c", j=PACK)[:, :, c0:c1])
            return raw

        xw, xs = table_tiles("x", x_words)
        ew, es = table_tiles("e", e_words)
        ab_rows = sb("ab_rows", [P, P], F32)
        nc.vector.memset(ab_rows[:], 0.0)
        ones = sb("ones", [P, P], F32)
        nc.vector.memset(ones[:], 1.0)
        column = sb("column", [P, P], F32)
        nc.vector.tensor_tensor_scan(column[:], ones[:], ones[:], -1.0, ALU.mult, ALU.add)
        turned = sb("turned", [P, P], F32)
        nc.vector.transpose(turned[:], column[:])
        ident = sb("ident", [P, P], F32)
        for q in range(4):
            rows = slice(32 * q, 32 * q + 32)
            nc.vector.tensor_scalar(ident[rows, :], column[rows, :], turned[rows, 32 * q : 32 * q + 1], None, ALU.is_equal)

        l_offs = load_list("l_offs", offs)
        load_words(xw, x_words)
        load_scales(xs, x_scales)
        l_far = load_list("l_far", far)
        w1_raw = load_weight("w1_raw", w1, 0, K)
        nc.sync.dma_start(out=ab_rows[0:TILES, :], in_=al[0:1, :].rearrange("o (t c) -> (o t) c", c=P))
        nc.sync.dma_start(out=ab_rows[TILES : 2 * TILES, :], in_=be[0:1, :].rearrange("o (t c) -> (o t) c", c=P))
        l_fine = load_list("l_fine", fine)
        load_words(ew, e_words)
        load_scales(es, e_scales)
        l_ffar = load_list("l_ffar", ffar)
        w2_raw = [load_weight("w2_raw%d" % h, w2, h * HALF, (h + 1) * HALF) for h in range(2)]
        w3_raw = [load_weight("w3_raw%d" % h, w3, h * HALF, (h + 1) * HALF) for h in range(2)]

        ab_ps = bank("prod0")
        nc.tensor.transpose(ab_ps[:, 0:P], ab_rows[:], ident[:])
        far_wt = sb("far_wt", [P, 2 * TILES], F32)
        near_wt = sb("near_wt", [P, 2 * TILES], F32)
        nc.scalar.copy(far_wt[:], ab_ps[:, 0 : 2 * TILES])
        nc.scalar.activation(near_wt[:], ab_ps[:, 0 : 2 * TILES], ACT.Copy, bias=1.0, scale=-1.0)

        def gather_words(name, wt, lt, j0, j1, tag=None):
            gw = sb("%s_w%d" % (name, j0), [P, j1 - j0], U32, tag)
            nc.vector.tensor_copy(gw[:], wt[:].bitcast(U32).indirect(lt[:, j0 // 16 : j1 // 16]))
            return gw

        def gather_bytes(name, st, lt, j0, j1, tag=None):
            gs = sb("%s_s%d" % (name, j0), [P, j1 - j0], U8, tag)
            nc.vector.tensor_copy(gs[:], st[:].indirect(lt[:, j0 // 16 : j1 // 16]))
            return gs

        def quantize(name, src, cols, tag=None):
            codes = sb(name + "_codes", [P, cols], U32, tag)
            scales = sb(name + "_bytes", [P, cols], U8)
            nc.vector.quantize_mx(out=codes[:].bitcast(FP8X4), scales=scales[:], in_=src)
            return codes, scales

        def round_on_gpsimd(dst, src):
            nc.gpsimd.tensor_scalar(dst, src, 1.0, 0.0, ALU.mult, ALU.add)

        def half_columns(wb, h):
            return wb[:, h * HALF * PACK : (h + 1) * HALF * PACK]

        picked = {}
        picked["y", 0] = (gather_words("y", xw, l_offs, 0, S), gather_bytes("y", xs, l_offs, 0, S))
        yf_words = gather_words("yf", xw, l_far, 0, S)
        w1_b = sb("w1_b", [P, K * PACK], BF16)
        nc.scalar.copy(
            half_columns(w1_b, 0).rearrange("p (c i j) -> p c j i", i=4, j=PACK),
            w1_raw[:, :, 0:HALF].rearrange("p j (c i) -> p c j i", i=4),
        )
        round_on_gpsimd(half_columns(w1_b, 1).rearrange("p (c j) -> p c j", j=PACK), w1_raw[:, :, HALF:K].rearrange("p j c -> p c j"))
        w1_q = quantize("w1", w1_b[:], K)
        picked["yf", 0] = (yf_words, gather_bytes("yf", xs, l_far, 0, S, "w1_b"))
        picked["p", 0] = (gather_words("p", ew, l_fine, 0, S), gather_bytes("p", es, l_fine, 0, S))
        pf_words = gather_words("pf", ew, l_ffar, 0, S)
        w2_b = sb("w2_b", [P, K * PACK], BF16)
        for h in range(2):
            round_on_gpsimd(half_columns(w2_b, h).rearrange("p (c j) -> p c j", j=PACK), w2_raw[h][:].rearrange("p j c -> p c j"))
        w2_q = quantize("w2", w2_b[:], K)
        picked["pf", 0] = (pf_words, gather_bytes("pf", es, l_ffar, 0, S, "w2_b"))

        def product(name, wq, t, tag):
            j0 = max(j for n, j in picked if n == name and j <= t * P)
            gw, gs = picked[name, j0]
            cols = slice(t * P - j0, (t + 1) * P - j0)
            acc = bank(tag)
            nc.tensor.matmul_mx(
                out=acc[:], lhsT=gw[:, cols].bitcast(FP8X4), lhsT_scale=gs[:, cols],
                rhs=wq[0][:].bitcast(FP8X4), rhs_scale=wq[1][:], start=True, stop=True,
            )
            return acc[:].rearrange("p (m r) -> p r m", r=PACK)

        def scaled(name, wq, wt, t, tag, term=None):
            acc = product(name, wq, t, tag)
            if term is None:
                term = sb("%s_term%d" % (name, t), [P, PACK, P], F32)[:]
            nc.scalar.activation(term, acc, ACT.Copy, scale=wt)
            return term

        def scaled_onto(name, wq, wt, t, tag, other, term):
            acc = product(name, wq, t, tag)
            nc.vector.scalar_tensor_tensor(term, acc, wt, other, ALU.mult, ALU.add)
            return term

        def turn_into(acc, term, first, last):
            for r in range(PACK):
                nc.tensor.matmul(
                    acc[:, r * P : (r + 1) * P], lhsT=term[:, r, :], rhs=ident[:], is_transpose=True,
                    start=(first and r == 0), stop=(last and r == PACK - 1),
                )

        out_codes = sb("out_codes", [P, S], I32)
        out_bytes = sb("out_bytes", [P, S], U8)
        out_rows = out_0.rearrange("(p r) j -> p r j", r=PACK)
        out_words = out_1[0].rearrange("p c r -> p (c r)").bitcast(I32)

        res_b = [sb("res_b%d" % h, [P, 2, P * PACK], BF16) for h in range(2)]
        sums = {}
        near = {}
        other = {}
        h_q = {}
        w3_q = []

        def hidden(t):
            hb = sb("h_b%d" % t, [P, P, PACK], BF16)
            nc.scalar.activation(hb[:], sums[t][:].rearrange("p (r j) -> p j r", r=PACK), ACT.Relu)
            h_bytes = sb("h_bytes%d" % t, [P, P], U8)
            nc.vector.quantize_mx(out=h_codes[t].bitcast(FP8X4), scales=h_bytes[:], in_=hb[:].rearrange("p j r -> p (j r)"))
            h_q[t] = (h_codes[t], h_bytes[:])

        def last(t):
            acc = bank("sum%d" % t)
            for r in range(PACK):
                cols = slice(r * P, (r + 1) * P)
                nc.tensor.matmul_mx(
                    out=acc[:, cols], lhsT=w3_q[0][:, cols].bitcast(FP8X4), lhsT_scale=w3_q[1][:, cols],
                    rhs=h_q[t][0].bitcast(FP8X4), rhs_scale=h_q[t][1], start=True, stop=True,
                )
            res = sb("res%d" % t, [P, PACK, P], F32)
            nc.scalar.copy(res[:].rearrange("p r j -> p (r j)"), acc[:])
            cols = slice(t * P, (t + 1) * P)
            nc.sync.dma_start(out=out_rows[:, :, cols], in_=res[:])
            rb = res_b[t // 2]
            nc.vector.tensor_copy(
                rb[:, t % 2].rearrange("p (c i r) -> p c r i", i=4, r=PACK), res[:].rearrange("p r (c i) -> p c r i", i=4)
            )
            if t % 2 == 1:
                pair = slice((t - 1) * P, (t + 1) * P)
                nc.vector.quantize_mx(
                    out=out_codes[:, pair].bitcast(FP8X4), scales=out_bytes[:, pair], in_=rb[:].rearrange("p a n -> p (a n)")
                )
                nc.sync.dma_start(out=out_words[:, pair], in_=out_codes[:, pair])

        def y_wt(t):
            return near_wt[:, t : t + 1]

        def yf_wt(t):
            return far_wt[:, t : t + 1]

        def p_wt(t):
            return near_wt[:, TILES + t : TILES + t + 1]

        def pf_wt(t):
            return far_wt[:, TILES + t : TILES + t + 1]

        for t in range(2):
            near[t] = scaled("y", w1_q, y_wt(t), t, "sum%d" % t)
        for t in range(2):
            other[t] = scaled("yf", w1_q, yf_wt(t), t, "sum%d" % (2 + t))
        for t in range(2, TILES):
            near[t] = scaled("y", w1_q, y_wt(t), t, "prod%d" % (2 * t - 4))
            other[t] = scaled("yf", w1_q, yf_wt(t), t, "prod%d" % (2 * t - 3))

        def coarse_sum(t):
            sums[t] = bank("sum%d" % t)
            turn_into(sums[t], near[t], True, False)
            turn_into(sums[t], other[t], False, False)

        for t in range(2):
            coarse_sum(t)

        w3_b = sb("w3_b", [P, PACK, 2, P // 2, PACK], BF16)
        for r in range(PACK):
            round_on_gpsimd(w3_b[:, r, 0], w3_raw[0][:].rearrange("p j (m r) -> p r m j", r=PACK)[:, r])
        nc.vector.tensor_copy(w3_b[:, :, 1].rearrange("p r m j -> p m j r"), w3_raw[1][:].rearrange("p j (m r) -> p m j r", r=PACK))

        fine_near = {}
        fused = {}
        fine_sums = sb("fine_sums", [P, TILES, PACK, P], F32, "w3_raw1")

        def fine_pair(t0):
            for t in (t0, t0 + 1):
                fine_near[t] = scaled("p", w2_q, p_wt(t), t, "prod%d" % (t % 2))
            for t in (t0, t0 + 1):
                fused[t] = scaled_onto("pf", w2_q, pf_wt(t), t, "prod%d" % (2 + t % 2), fine_near[t], fine_sums[:, t])

        fine_pair(0)
        for t in range(2, TILES):
            coarse_sum(t)
        fine_pair(2)
        w3_q.extend(quantize("w3", w3_b[:].rearrange("p r h m j -> p (r h m j)"), K))
        h_codes = [sb("h_codes0", [P, P], U32)[:]]
        h_later = sb("h_later", [P, TILES - 1, P], U32, "w3_b")
        h_codes.extend([h_later[:, t] for t in range(TILES - 1)])
        for t in range(TILES):
            turn_into(sums[t], fused[t], False, True)
        for t in range(TILES):
            hidden(t)
        for t in range(TILES):
            last(t)

        for q in range(4):
            eng = nc.sync if q % 2 == 0 else nc.scalar
            eng.dma_start(out=out_2[0, 4 * q : 4 * q + 4, :].bitcast(I32), in_=out_bytes[32 * q : 32 * q + 4, :].bitcast(I32))
